import numpy as np
import ml_dtypes

BF16 = ml_dtypes.bfloat16


def bf(x):
    return np.asarray(x, np.float32).astype(BF16)


def f32(x):
    return np.asarray(x, np.float32)


def f64(x):
    return np.asarray(x).astype(np.float64)


def striped(idx):
    return np.concatenate([l.reshape(-1, 16).T for l in idx])


def rows(idx, k):
    return np.tile(np.repeat(idx, 16, axis=0), (k // (16 * 8), 1))


def look(tab, idx):
    return np.take_along_axis(f64(tab), rows(idx, len(tab)), axis=1)


K, S, V, N, M = 256, 2048, 1024, 1024, 512


def setup_inputs():
    return {"tab": f32(np.random.standard_normal((K, S))), "w": bf(np.random.standard_normal((K, M)) / np.sqrt(K)), "offs": striped(np.random.randint(0, S, (8, N)))}


def reference(tab, w, offs):
    idx = np.stack([g.T.reshape(-1) for g in np.split(offs, 8)])
    t = look(tab, idx)
    x = np.minimum(np.maximum(t, -1.25), 1.0)
    y = f64(w).T @ x
    return y

@@ -1,0 +1,69 @@
+import concourse.mybir as mybir
+
+F32 = mybir.dt.float32
+BF16 = mybir.dt.bfloat16
+U16 = mybir.dt.uint16
+MAX = mybir.AluOpType.max
+MIN = mybir.AluOpType.min
+
+P = 128
+ROWS = 256
+CODES = 2048
+N = 1024
+M = 512
+PIECE = 512
+LOW, HIGH = -1.25, 1.0
+
+FLOPS = 2 * ROWS * M * N
+
+
+def tile_lookup_deq_clip_none_kernel(tc, tab, w, offs, out):
+    nc = tc.nc
+    blocks = ROWS // P
+    pieces = N // PIECE
+    row_blocks = M // P
+    with (
+        tc.tile_pool(name="held", bufs=1) as held,
+        tc.psum_pool(name="sums", bufs=1) as sums,
+    ):
+        offsets = held.tile([P, N // 16], U16, name="offsets")
+        nc.sync.dma_start(offsets[:], offs)
+
+        windows, weights = [], []
+        for b in range(blocks):
+            window = held.tile([P, CODES], F32, name=f"window{b}")
+            nc.sync.dma_start(window[:], tab[b * P : (b + 1) * P, :])
+            windows.append(window)
+            weight = held.tile([P, M], BF16, name=f"weight{b}")
+            nc.sync.dma_start(weight[:], w[b * P : (b + 1) * P, :])
+            weights.append(weight)
+
+        banks = {}
+        for c in range(pieces):
+            for m in range(row_blocks):
+                banks[c, m] = sums.tile([P, PIECE], F32, name=f"bank{c}_{m}")
+
+        for b in range(blocks):
+            for c in range(pieces):
+                codes = offsets[:, c * PIECE // 16 : (c + 1) * PIECE // 16]
+                clamped = held.tile([P, PIECE], F32, name=f"clamped{b}_{c}")
+                nc.vector.tensor_scalar(clamped[:], windows[b][:].indirect(codes), LOW, HIGH, op0=MAX, op1=MIN)
+                x = held.tile([P, PIECE], BF16, name=f"x{b}_{c}")
+                nc.scalar.copy(x[:], clamped[:])
+                for m in range(row_blocks):
+                    nc.tensor.matmul(
+                        banks[c, m][:],
+                        weights[b][:, m * P : (m + 1) * P],
+                        x[:],
+                        start=(b == 0),
+                        stop=(b == blocks - 1),
+                    )
+
+        for c in range(pieces):
+            for m in range(row_blocks):
+                result = held.tile([P, PIECE], F32, name=f"result{c}_{m}")
+                if m % 2 == 0:
+                    nc.scalar.copy(result[:], banks[c, m][:])
+                else:
+                    nc.vector.tensor_copy(result[:], banks[c, m][:])
+                nc.sync.dma_start(out[m * P : (m + 1) * P, c * PIECE : (c + 1) * PIECE], result[:])

@@ -13,6 +13,7 @@ N = 1024
 M = 512
 PIECE = 512
 LOW, HIGH = -1.25, 1.0
+WARM_UPS = 12
 
 FLOPS = 2 * ROWS * M * N
 
@@ -42,6 +43,11 @@ def tile_lookup_deq_clip_none_kernel(tc, tab, w, offs, out):
         for c in range(pieces):
             for m in range(row_blocks):
                 banks[c, m] = sums.tile([P, PIECE], F32, name=f"bank{c}_{m}")
+
+        zeros = held.tile([P, PIECE], BF16, name="zeros")
+        nc.vector.memset(zeros[:], 0.0)
+        for repeat in range(WARM_UPS):
+            nc.tensor.matmul(banks[0, 0][:], zeros[:, :P], zeros[:], start=True, stop=True)
 
         for b in range(blocks):
             for c in range(pieces):

@@ -55,7 +55,8 @@ def tile_lookup_deq_clip_none_kernel(tc, tab, w, offs, out):
                 clamped = held.tile([P, PIECE], F32, name=f"clamped{b}_{c}")
                 nc.vector.tensor_scalar(clamped[:], windows[b][:].indirect(codes), LOW, HIGH, op0=MAX, op1=MIN)
                 x = held.tile([P, PIECE], BF16, name=f"x{b}_{c}")
-                nc.scalar.copy(x[:], clamped[:])
+                nc.scalar.copy(x[:, : PIECE // 2], clamped[:, : PIECE // 2])
+                nc.gpsimd.tensor_copy(x[:, PIECE // 2 :], clamped[:, PIECE // 2 :])
                 for m in range(row_blocks):
                     nc.tensor.matmul(
                         banks[c, m][:],

import concourse.mybir as mybir

F32 = mybir.dt.float32
BF16 = mybir.dt.bfloat16
U16 = mybir.dt.uint16
MAX = mybir.AluOpType.max
MIN = mybir.AluOpType.min

P = 128
ROWS = 256
CODES = 2048
N = 1024
M = 512
PIECE = 512
LOW, HIGH = -1.25, 1.0
WARM_UPS = 12

FLOPS = 2 * ROWS * M * N


def tile_lookup_deq_clip_none_kernel(tc, tab, w, offs, out):
    nc = tc.nc
    blocks = ROWS // P
    pieces = N // PIECE
    row_blocks = M // P
    with (
        tc.tile_pool(name="held", bufs=1) as held,
        tc.psum_pool(name="sums", bufs=1) as sums,
    ):
        offsets = held.tile([P, N // 16], U16, name="offsets")
        nc.sync.dma_start(offsets[:], offs)

        windows, weights = [], []
        for b in range(blocks):
            window = held.tile([P, CODES], F32, name=f"window{b}")
            nc.sync.dma_start(window[:], tab[b * P : (b + 1) * P, :])
            windows.append(window)
            weight = held.tile([P, M], BF16, name=f"weight{b}")
            nc.sync.dma_start(weight[:], w[b * P : (b + 1) * P, :])
            weights.append(weight)

        banks = {}
        for c in range(pieces):
            for m in range(row_blocks):
                banks[c, m] = sums.tile([P, PIECE], F32, name=f"bank{c}_{m}")

        zeros = held.tile([P, PIECE], BF16, name="zeros")
        nc.vector.memset(zeros[:], 0.0)
        for repeat in range(WARM_UPS):
            nc.tensor.matmul(banks[0, 0][:], zeros[:, :P], zeros[:], start=True, stop=True)

        for b in range(blocks):
            for c in range(pieces):
                codes = offsets[:, c * PIECE // 16 : (c + 1) * PIECE // 16]
                clamped = held.tile([P, PIECE], F32, name=f"clamped{b}_{c}")
                nc.vector.tensor_scalar(clamped[:], windows[b][:].indirect(codes), LOW, HIGH, op0=MAX, op1=MIN)
                x = held.tile([P, PIECE], BF16, name=f"x{b}_{c}")
                nc.scalar.copy(x[:, : PIECE // 2], clamped[:, : PIECE // 2])
                nc.gpsimd.tensor_copy(x[:, PIECE // 2 :], clamped[:, PIECE // 2 :])
                for m in range(row_blocks):
                    nc.tensor.matmul(
                        banks[c, m][:],
                        weights[b][:, m * P : (m + 1) * P],
                        x[:],
                        start=(b == 0),
                        stop=(b == blocks - 1),
                    )

        for c in range(pieces):
            for m in range(row_blocks):
                result = held.tile([P, PIECE], F32, name=f"result{c}_{m}")
                if m % 2 == 0:
                    nc.scalar.copy(result[:], banks[c, m][:])
                else:
                    nc.vector.tensor_copy(result[:], banks[c, m][:])
                nc.sync.dma_start(out[m * P : (m + 1) * P, c * PIECE : (c + 1) * PIECE], result[:])
